import numpy as np
import ml_dtypes


def mxq(x, axis, fmt="e4m3"):
    dtype, down = {"e4m3": (ml_dtypes.float8_e4m3fn, 7), "e5m2": (ml_dtypes.float8_e5m2, 14)}[fmt]
    v = np.moveaxis(np.asarray(x, np.float32).astype(ml_dtypes.bfloat16).astype(np.float64), axis, -1)
    blocks = v.reshape(v.shape[:-1] + (-1, 32))
    amax = np.abs(blocks).max(-1, keepdims=True)
    byte = np.maximum(np.where(amax > 0, np.frexp(amax)[1] - 1 + 127, 0) - down, 1)
    scale = np.exp2(byte - 127.0)
    codes = (blocks / scale).astype(np.float32).astype(dtype).astype(np.float64)
    return np.moveaxis((codes * scale).reshape(v.shape), -1, axis)


WIDE = False


def mx_kscale(k):
    if not WIDE:
        return np.ones(k)
    levels = np.array([10, -10, 5, -5, 0])
    if k % 512:
        return np.exp2(np.random.permutation(np.resize(levels, k // 32))).repeat(32)
    a = np.empty((k // 512, 16))
    for p in range(k // 512):
        a[p, :8] = np.random.permutation(np.resize(levels, 8))
        for g in range(8):
            far = levels[np.abs(levels - a[p, g]) >= 10]
            a[p, g + 8] = far[np.random.randint(len(far))]
    return np.exp2(a.ravel()).repeat(32)


def f64(x):
    return np.asarray(x).astype(np.float64)


def striped(idx):
    return np.tile(idx.reshape(-1, 16).T, (8, 1)).astype(np.uint16)


def unstriped(offs):
    return offs[:16].T.reshape(-1).astype(np.int64)


def pack_weight(w):
    k, n = w.shape
    w = f64(np.asarray(w, np.float32).astype(ml_dtypes.bfloat16)).reshape(k // 32, 32, n)
    amax = np.abs(w).max(1)
    byte = np.clip(np.where(amax > 0, np.frexp(amax)[1] - 1 + 127 - 7, 1), 1, 254)
    scaled = (w * np.exp2(127.0 - byte)[:, None, :]).reshape(k, n).astype(np.float32)
    words = np.ascontiguousarray(scaled.reshape(k // 512, 128, 4, n).transpose(0, 1, 3, 2)).astype(ml_dtypes.float8_e4m3fn).view(np.uint8)
    return words, np.ascontiguousarray(byte.astype(np.uint8).reshape(k // 512, 16, n))


def unpack_weight(words, scales):
    g, p, n, _ = words.shape
    vals = np.ascontiguousarray(words).view(ml_dtypes.float8_e4m3fn).astype(np.float64) * np.repeat(np.exp2(scales.astype(np.float64) - 127.0), 8, axis=1)[..., None]
    return vals.transpose(0, 1, 3, 2).reshape(g * 512, n)


E2M1 = np.array([0.0, 0.5, 1.0, 1.5, 2.0, 3.0, 4.0, 6.0, -0.0, -0.5, -1.0, -1.5, -2.0, -3.0, -4.0, -6.0])


def pack_fp4(w):
    k, n = w.shape
    w = f64(np.asarray(w, np.float32).astype(ml_dtypes.bfloat16)).reshape(k // 32, 32, n)
    amax = np.abs(w).max(1)
    mant, ex = np.frexp(amax / 6.0)
    byte = np.clip(np.where(amax > 0, np.where(mant > 0.5, ex, ex - 1) + 127, 1), 1, 254)
    scaled = (w * np.exp2(127.0 - byte)[:, None, :]).reshape(k, n).astype(np.float32)
    c = np.ascontiguousarray(scaled.reshape(k // 512, 128, 4, n).transpose(0, 1, 3, 2)).astype(ml_dtypes.float4_e2m1fn).view(np.uint8) & 0xF
    words = (c[..., 0::2] | (c[..., 1::2] << 4)).reshape(k // 512, 128, 2 * n)
    return np.ascontiguousarray(words), np.ascontiguousarray(byte.astype(np.uint8).reshape(k // 512, 16, n))


def unpack_fp4(words, scales):
    g, _, n = scales.shape
    words = np.ascontiguousarray(words).reshape(g, 128, n, 2)
    nib = np.empty((g, 128, n, 4), np.uint8)
    nib[..., 0::2] = words & 0xF
    nib[..., 1::2] = words >> 4
    vals = E2M1[nib] * np.repeat(np.exp2(scales.astype(np.float64) - 127.0), 8, axis=1)[..., None]
    return vals.transpose(0, 1, 3, 2).reshape(g * 512, n)


def sigmoid(v):
    return 1.0 / (1.0 + np.exp(-np.maximum(v, -700.0)))


K, T, S, N, H = 512, 2048, 512, 256, 512


def setup_inputs():
    n = np.random.standard_normal
    s = mx_kscale(K)[:, None]
    u = mx_kscale(H)
    packed_xT = pack_weight(n((K, T)) * s)
    packed_w1 = pack_fp4(n((K, H)) / np.sqrt(K) / s)
    packed_w2 = pack_fp4(n((K, H)) / np.sqrt(K) / s)
    packed_w3 = pack_fp4(n((H, N)) / np.sqrt(H) / u[:, None])
    return {
        "x_words": packed_xT[0],
        "x_scales": packed_xT[1],
        "w1_words": packed_w1[0],
        "w1_scales": packed_w1[1],
        "w2_words": packed_w2[0],
        "w2_scales": packed_w2[1],
        "ign": (1.5 * n((H, S))).astype(np.float32),
        "unit": (np.random.uniform(0.6, 1.4, (H, 1)) * u[:, None]).astype(np.float32),
        "w3_words": packed_w3[0],
        "w3_scales": packed_w3[1],
        "offs": striped(np.random.permutation(T)[:S]),
        "uw": striped(np.random.permutation(S)),
        "sd": striped(np.random.permutation(S)),
    }


def reference(x_words, x_scales, w1_words, w1_scales, w2_words, w2_scales, ign, unit, w3_words, w3_scales, offs, uw, sd):
    burn = sigmoid(f64(ign))
    iu = sigmoid(f64(ign)[:, unstriped(uw)])
    xq = unpack_weight(x_words, x_scales)[:, unstriped(offs)]
    wd = unpack_fp4(w2_words, w2_scales).T @ xq
    windf = np.exp(0.9 * np.tanh(wd))
    is_ = sigmoid(f64(ign)[:, unstriped(sd)])
    heat = iu * windf + 0.5 * is_
    fu = unpack_fp4(w1_words, w1_scales).T @ xq
    fuel = np.log(np.exp(fu) + 1.0) + 0.1
    spread = heat / (fuel + 0.3 * heat)
    bnew = np.maximum(burn, -1.0 * np.exp(-1.0 * spread) + 1.0)
    fb = fuel[:, unstriped(uw)]
    hid = f64(unit) * (bnew - burn + 0.2 * fb)
    return unpack_fp4(w3_words, w3_scales).T @ mxq(hid, 0, "e4m3")

@@ -1,0 +1,208 @@
+import math
+from contextlib import ExitStack
+
+import concourse.mybir as mybir
+
+K, T, S, N, H = 512, 2048, 512, 256, 512
+FLOPS = 2 * K * H * S * 2 + 2 * H * N * S
+
+F32 = mybir.dt.float32
+BF16 = mybir.dt.bfloat16
+I32 = mybir.dt.int32
+U32 = mybir.dt.uint32
+U16 = mybir.dt.uint16
+U8 = mybir.dt.uint8
+FP8X4 = mybir.dt.float8_e4m3fn_x4
+FP4X4 = mybir.dt.float4_e2m1fn_x4
+ALU = mybir.AluOpType
+ACT = mybir.ActivationFunctionType
+
+P = 128
+PACK = 4
+SPARE = 8
+HALF = S // 2
+CHUNKS = ((0, 128), (128, 256), (256, 384), (384, 512))
+TINY = 2.0 ** -60
+HUGE = 2.0 ** 60
+
+
+def load_scale_rows(queue, plane, rows):
+    for q in range(4):
+        queue.dma_start(out=plane[32 * q : 32 * q + 4, :].bitcast(I32), in_=rows[0, 4 * q : 4 * q + 4, :].bitcast(I32))
+
+
+def tile_picked_yfirefr_new_p_kernel(
+    tc, x_words, x_scales, w1_words, w1_scales, w2_words, w2_scales, ign, unit, w3_words, w3_scales, offs, uw, sd, out
+):
+    nc = tc.nc
+    with ExitStack() as ctx:
+        keep = ctx.enter_context(tc.tile_pool(name="keep", bufs=1))
+        psum = ctx.enter_context(tc.psum_pool(name="psum", bufs=1))
+
+        offs_t = keep.tile([P, S // 16], U16, name="offs_t")
+        uw_t = keep.tile([P, S // 16], U16, name="uw_t")
+        sd_t = keep.tile([P, S // 16], U16, name="sd_t")
+
+        xw = keep.tile([P, T], I32, name="xw", align_bytes=64)
+        xs = keep.tile([P, T], U8, name="xs", align_bytes=64)
+        w_raw = [keep.tile([P, 2 * H], U8, name="w_raw%d" % i, align_bytes=64) for i in range(2)]
+        ws_raw = [keep.tile([P, H], U8, name="ws_raw%d" % i, align_bytes=64) for i in range(2)]
+        w3w = keep.tile([P, 2 * N], U8, name="w3w", align_bytes=64)
+        w3s = keep.tile([P, N], U8, name="w3s", align_bytes=64)
+        ign_t = [keep.tile([P, 2, S], F32, name="ign%d" % i) for i in range(2)]
+        unit_t = keep.tile([P, PACK], F32, name="unit_t")
+        burn = [keep.tile([P, S + SPARE], F32, name="burn%d" % t) for t in range(PACK)]
+
+        nc.vector.memset(xs[:].bitcast(I32), 0)
+        nc.vector.memset(ws_raw[0][:].bitcast(I32), 0)
+        nc.vector.memset(ws_raw[1][:].bitcast(I32), 0)
+        nc.gpsimd.memset(w3s[:].bitcast(I32), 0)
+        for t in range(PACK):
+            nc.gpsimd.memset(burn[t][:, S:], 0.0)
+
+        ign_rows = ign.rearrange("(p t) s -> p t s", t=PACK)
+        nc.sync.dma_start(out=ign_t[0][:], in_=ign_rows[:, 0:2, :])
+        nc.sync.dma_start(out=w_raw[0][:], in_=w2_words[0])
+        nc.sync.dma_start(out=w_raw[1][:], in_=w1_words[0])
+        load_scale_rows(nc.sync, xs, x_scales)
+        nc.sync.dma_start(offs_t[:], offs)
+        nc.sync.dma_start(out=ign_t[1][:], in_=ign_rows[:, 2:4, :])
+        load_scale_rows(nc.sync, ws_raw[0], w2_scales)
+        nc.sync.dma_start(out=xw[:], in_=x_words[0].rearrange("p n t -> p (n t)").bitcast(I32))
+        load_scale_rows(nc.sync, ws_raw[1], w1_scales)
+        nc.sync.dma_start(uw_t[:], uw)
+        nc.sync.dma_start(sd_t[:], sd)
+        nc.sync.dma_start(out=unit_t[:], in_=unit.rearrange("(p t) o -> p (t o)", t=PACK))
+        nc.sync.dma_start(out=w3w[:], in_=w3_words[0])
+        load_scale_rows(nc.sync, w3s, w3_scales)
+
+        for t in range(PACK):
+            nc.scalar.activation(burn[t][:, :S], ign_t[t // 2][:, t % 2, :], ACT.Sigmoid)
+
+        w_dealt = [keep.tile([P, 2 * H], U8, name="w_dealt%d" % i, align_bytes=64) for i in range(2)]
+        ws_dealt = [keep.tile([P, H], U8, name="ws_dealt%d" % i, align_bytes=64) for i in range(2)]
+        xg_w = keep.tile([P, S], U32, name="xg_w", align_bytes=64)
+        xg_s = keep.tile([P, S], U8, name="xg_s", align_bytes=64)
+
+        def deal_words(i):
+            nc.vector.tensor_copy(
+                out=w_dealt[i][:].rearrange("p (t m b) -> p m t b", t=PACK, b=2),
+                in_=w_raw[i][:].rearrange("p (m t b) -> p m t b", t=PACK, b=2),
+            )
+
+        def deal_scales(i):
+            nc.vector.tensor_copy(
+                out=ws_dealt[i][:].rearrange("p (t m) -> p m t", t=PACK),
+                in_=ws_raw[i][:].rearrange("p (m t) -> p m t", t=PACK),
+            )
+
+        deal_words(0)
+        deal_words(1)
+        nc.vector.tensor_copy(xg_s[:], xs[:].indirect(offs_t[:]))
+        deal_scales(0)
+        deal_scales(1)
+        nc.vector.tensor_copy(xg_w[:], xw[:].bitcast(U32).indirect(offs_t[:]))
+
+        def first_product(i, t, tag):
+            acc = psum.tile([P, S], F32, name=tag, tag=tag)
+            nc.tensor.matmul_mx(
+                out=acc[:],
+                lhsT=w_dealt[i][:, 2 * P * t : 2 * P * (t + 1)].bitcast(FP4X4),
+                lhsT_scale=ws_dealt[i][:, P * t : P * (t + 1)],
+                rhs=xg_w[:].bitcast(FP8X4),
+                rhs_scale=xg_s[:],
+                start=True,
+                stop=True,
+            )
+            return acc
+
+        wd = [first_product(0, t, "bank%d" % t) for t in range(2)]
+        fu = [first_product(1, t, "bank%d" % (PACK + t)) for t in range(PACK)]
+        wd.extend([first_product(0, t, "bank%d" % t) for t in range(2, PACK)])
+
+        burn5 = keep.tile([P, PACK, S], F32, name="burn5")
+        for t in range(PACK):
+            nc.vector.tensor_scalar(burn5[:, t, :], burn[t][:, :S], 5.0, -5.0, ALU.mult, ALU.add)
+        gain = keep.tile([P, PACK], F32, name="gain")
+        nc.vector.tensor_scalar(gain[:], unit_t[:], -0.2, None, ALU.mult)
+
+        tw = keep.tile([P, PACK, S], F32, name="tw")
+        wind2 = keep.tile([P, PACK, S], F32, name="wind2")
+        upwind = keep.tile([P, PACK, S], F32, name="upwind")
+        heat2 = keep.tile([P, PACK, S], F32, name="heat2")
+
+        def heat_rows(t):
+            nc.scalar.activation(tw[:, t, :], wd[t][:], ACT.Tanh)
+            nc.scalar.activation(wind2[:, t, :], tw[:, t, :], ACT.Exp, bias=math.log(2.0), scale=0.9)
+            nc.vector.tensor_tensor(upwind[:, t, :], burn[t][:].indirect(uw_t[:]), wind2[:, t, :], ALU.mult)
+            nc.vector.tensor_tensor(heat2[:, t, :], burn[t][:].indirect(sd_t[:]), upwind[:, t, :], ALU.add)
+
+        efu = keep.tile([P, PACK, S], F32, name="efu")
+        efu_c = keep.tile([P, PACK, S], F32, name="efu_c")
+        soft = keep.tile([P, PACK, S], F32, name="soft")
+        fuel = keep.tile([P, PACK, S], F32, name="fuel")
+        log_heat = keep.tile([P, PACK, S], F32, name="log_heat")
+        log_fuel = keep.tile([P, PACK, S], F32, name="log_fuel")
+        fb = keep.tile([P, PACK, HALF], F32, name="fb")
+        heat_rows(0)
+        heat_rows(1)
+        for t in range(PACK):
+            nc.scalar.activation(efu[:, t, :], fu[t][:], ACT.Exp)
+        nc.vector.tensor_scalar(efu_c[:], efu[:], HUGE, None, ALU.min)
+        heat_rows(2)
+        heat_rows(3)
+        for t in range(PACK):
+            nc.scalar.activation(soft[:, t, :], efu_c[:, t, :], ACT.Ln, bias=math.exp(0.1), scale=math.exp(0.1))
+            nc.vector.scalar_tensor_tensor(fuel[:, t, :], fu[t][:], 0.1, soft[:, t, :], ALU.add, ALU.max)
+        for t in range(PACK):
+            nc.scalar.activation(log_heat[:, t, :], heat2[:, t, :], ACT.Ln, bias=TINY, scale=0.15)
+        for t in range(PACK):
+            nc.scalar.activation(log_fuel[:, t, :], fuel[:, t, :], ACT.Ln)
+        for t in range(PACK):
+            nc.vector.tensor_copy(fb[:, t, :], fuel[:, t, :].indirect(uw_t[:, : HALF // 16]))
+
+        logit = keep.tile([P, PACK, S], F32, name="logit")
+        for lo, hi in CHUNKS:
+            nc.vector.tensor_tensor(logit[:, :, lo:hi], log_heat[:, :, lo:hi], log_fuel[:, :, lo:hi], ALU.subtract)
+
+        out_rows = out.rearrange("(a p) s -> p a s", p=P)
+        tzs = []
+        for c, (lo, hi) in enumerate(CHUNKS):
+            w = hi - lo
+            tz = keep.tile([P, PACK, w], F32, name="tz%d" % c)
+            tzs.append(tz)
+            miss5 = keep.tile([P, PACK, w], F32, name="miss5_%d" % c)
+            short5 = keep.tile([P, PACK, w], F32, name="short5_%d" % c)
+            total = keep.tile([P, PACK, w], F32, name="total%d" % c)
+            hid = keep.tile([P, w, PACK], BF16, name="hid%d" % c, align_bytes=64)
+            codes = keep.tile([P, w], U32, name="codes%d" % c, align_bytes=64)
+            scales = keep.tile([P, w], U8, name="scales%d" % c, align_bytes=64)
+            res = keep.tile([P, N // P, w], F32, name="res%d" % c)
+            if lo >= HALF:
+                for t in range(PACK):
+                    nc.scalar.activation(tzs[c - 2][:, t, :], fuel[:, t, :].indirect(uw_t[:, lo // 16 : hi // 16]), ACT.Copy)
+            nc.scalar.activation(tz[:], logit[:, :, lo:hi], ACT.Tanh, scale=0.5)
+            nc.scalar.activation(miss5[:], tz[:], ACT.Exp, bias=math.log(5.0) - 0.5 / 0.3, scale=-0.5 / 0.3)
+            nc.vector.tensor_tensor(short5[:], miss5[:], burn5[:, :, lo:hi], ALU.add)
+            fb_c = tzs[c - 2][:] if lo >= HALF else fb[:, :, lo:hi]
+            nc.vector.scalar_tensor_tensor(total[:], short5[:], 0.0, fb_c, ALU.min, ALU.subtract)
+            nc.vector.tensor_tensor(
+                hid[:].rearrange("p (c i) t -> p c t i", i=4),
+                total[:].rearrange("p t (c i) -> p c t i", i=4),
+                gain[:].unsqueeze(1).unsqueeze(3).to_broadcast([P, w // 4, PACK, 4]),
+                ALU.mult,
+            )
+            nc.vector.quantize_mx(out=codes[:].bitcast(FP8X4), scales=scales[:], in_=hid[:].rearrange("p c t -> p (c t)"))
+            acc = psum.tile([P, N // P, w], F32, name="acc%d" % c, tag="bank%d" % c)
+            for a in range(N // P):
+                nc.tensor.matmul_mx(
+                    out=acc[:, a, :],
+                    lhsT=w3w[:, 2 * P * a : 2 * P * (a + 1)].bitcast(FP4X4),
+                    lhsT_scale=w3s[:, P * a : P * (a + 1)],
+                    rhs=codes[:].bitcast(FP8X4),
+                    rhs_scale=scales[:],
+                    start=True,
+                    stop=True,
+                )
+            nc.scalar.copy(res[:], acc[:])
+            nc.sync.dma_start(out=out_rows[:, :, lo:hi], in_=res[:])

@@ -26,11 +26,6 @@ TINY = 2.0 ** -60
 HUGE = 2.0 ** 60
 
 
-def load_scale_rows(queue, plane, rows):
-    for q in range(4):
-        queue.dma_start(out=plane[32 * q : 32 * q + 4, :].bitcast(I32), in_=rows[0, 4 * q : 4 * q + 4, :].bitcast(I32))
-
-
 def tile_picked_yfirefr_new_p_kernel(
     tc, x_words, x_scales, w1_words, w1_scales, w2_words, w2_scales, ign, unit, w3_words, w3_scales, offs, uw, sd, out
 ):
@@ -39,48 +34,64 @@ def tile_picked_yfirefr_new_p_kernel(
         keep = ctx.enter_context(tc.tile_pool(name="keep", bufs=1))
         psum = ctx.enter_context(tc.psum_pool(name="psum", bufs=1))
 
+        reuse = ctx.enter_context(tc.tile_pool(name="reuse", bufs=1))
+
+        def load_scale_rows(plane, rows, quadrants):
+            for q in quadrants:
+                nc.sync.dma_start(out=plane[32 * q : 32 * q + 4, :].bitcast(I32), in_=rows[0, 4 * q : 4 * q + 4, :].bitcast(I32))
+
         offs_t = keep.tile([P, S // 16], U16, name="offs_t")
         uw_t = keep.tile([P, S // 16], U16, name="uw_t")
         sd_t = keep.tile([P, S // 16], U16, name="sd_t")
 
-        xw = keep.tile([P, T], I32, name="xw", align_bytes=64)
+        xw = reuse.tile([P, T], I32, name="xw", offset=0, align_bytes=64)
         xs = keep.tile([P, T], U8, name="xs", align_bytes=64)
         w_raw = [keep.tile([P, 2 * H], U8, name="w_raw%d" % i, align_bytes=64) for i in range(2)]
         ws_raw = [keep.tile([P, H], U8, name="ws_raw%d" % i, align_bytes=64) for i in range(2)]
         w3w = keep.tile([P, 2 * N], U8, name="w3w", align_bytes=64)
         w3s = keep.tile([P, N], U8, name="w3s", align_bytes=64)
-        ign_t = [keep.tile([P, 2, S], F32, name="ign%d" % i) for i in range(2)]
+        ign_t = keep.tile([P, PACK, S], F32, name="ign_t")
         unit_t = keep.tile([P, PACK], F32, name="unit_t")
-        burn = [keep.tile([P, S + SPARE], F32, name="burn%d" % t) for t in range(PACK)]
+        burn = [keep.tile([P, S + SPARE], F32, name="burn%d" % t) for t in range(2)]
+        burn.extend(
+            [reuse.tile([P, S + SPARE], F32, name="burn%d" % t, offset=H + (t - 2) * 2112, align_bytes=64) for t in range(2, PACK)]
+        )
 
-        nc.vector.memset(xs[:].bitcast(I32), 0)
+        nc.gpsimd.memset(xs[:].bitcast(I32), 0)
         nc.vector.memset(ws_raw[0][:].bitcast(I32), 0)
         nc.vector.memset(ws_raw[1][:].bitcast(I32), 0)
-        nc.gpsimd.memset(w3s[:].bitcast(I32), 0)
-        for t in range(PACK):
-            nc.gpsimd.memset(burn[t][:, S:], 0.0)
+        nc.vector.memset(w3s[:].bitcast(I32), 0)
+        for t in range(2):
+            nc.vector.memset(burn[t][:, S:], 0.0)
 
-        ign_rows = ign.rearrange("(p t) s -> p t s", t=PACK)
-        nc.sync.dma_start(out=ign_t[0][:], in_=ign_rows[:, 0:2, :])
-        nc.sync.dma_start(out=w_raw[0][:], in_=w2_words[0])
-        nc.sync.dma_start(out=w_raw[1][:], in_=w1_words[0])
-        load_scale_rows(nc.sync, xs, x_scales)
         nc.sync.dma_start(offs_t[:], offs)
-        nc.sync.dma_start(out=ign_t[1][:], in_=ign_rows[:, 2:4, :])
-        load_scale_rows(nc.sync, ws_raw[0], w2_scales)
-        nc.sync.dma_start(out=xw[:], in_=x_words[0].rearrange("p n t -> p (n t)").bitcast(I32))
-        load_scale_rows(nc.sync, ws_raw[1], w1_scales)
-        nc.sync.dma_start(uw_t[:], uw)
         nc.sync.dma_start(sd_t[:], sd)
+        nc.sync.dma_start(out=w_raw[0][:], in_=w2_words[0])
+        nc.sync.dma_start(out=ign_t[:], in_=ign.rearrange("(p t) s -> p t s", t=PACK))
+        load_scale_rows(xs, x_scales, range(4))
+        load_scale_rows(ws_raw[0], w2_scales, range(2))
+        nc.sync.dma_start(out=xw[:], in_=x_words[0].rearrange("p n t -> p (n t)").bitcast(I32))
+        load_scale_rows(ws_raw[0], w2_scales, range(2, 4))
+        nc.sync.dma_start(out=w_raw[1][:], in_=w1_words[0])
+        load_scale_rows(ws_raw[1], w1_scales, range(4))
+        nc.sync.dma_start(uw_t[:], uw)
         nc.sync.dma_start(out=unit_t[:], in_=unit.rearrange("(p t) o -> p (t o)", t=PACK))
         nc.sync.dma_start(out=w3w[:], in_=w3_words[0])
-        load_scale_rows(nc.sync, w3s, w3_scales)
+        load_scale_rows(w3s, w3_scales, range(4))
 
-        for t in range(PACK):
-            nc.scalar.activation(burn[t][:, :S], ign_t[t // 2][:, t % 2, :], ACT.Sigmoid)
+        th = keep.tile([P, PACK, S], F32, name="th")
+        th_flat = th[:].rearrange("p t s -> p (t s)")
+        side = [keep.tile([P, S], F32, name="side%d" % t) for t in range(2)]
+        for i in range(2):
+            nc.scalar.activation(th[:, 2 * i : 2 * i + 2, :], ign_t[:, 2 * i : 2 * i + 2, :], ACT.Tanh, scale=0.5)
+        for t in range(2):
+            nc.scalar.activation(side[t][:], th_flat[:, S * t : S * (t + 2)].indirect(sd_t[:]), ACT.Copy, bias=0.5, scale=0.5)
 
         w_dealt = [keep.tile([P, 2 * H], U8, name="w_dealt%d" % i, align_bytes=64) for i in range(2)]
-        ws_dealt = [keep.tile([P, H], U8, name="ws_dealt%d" % i, align_bytes=64) for i in range(2)]
+        ws_dealt = [
+            keep.tile([P, H], U8, name="ws_dealt0", align_bytes=64),
+            reuse.tile([P, H], U8, name="ws_dealt1", offset=0, align_bytes=64),
+        ]
         xg_w = keep.tile([P, S], U32, name="xg_w", align_bytes=64)
         xg_s = keep.tile([P, S], U8, name="xg_s", align_bytes=64)
 
@@ -97,11 +108,13 @@ def tile_picked_yfirefr_new_p_kernel(
             )
 
         deal_words(0)
-        deal_words(1)
         nc.vector.tensor_copy(xg_s[:], xs[:].indirect(offs_t[:]))
+        for t in range(2):
+            nc.vector.tensor_scalar(burn[t][:, :S], th[:, t, :], 0.5, 0.5, ALU.mult, ALU.add)
         deal_scales(0)
-        deal_scales(1)
         nc.vector.tensor_copy(xg_w[:], xw[:].bitcast(U32).indirect(offs_t[:]))
+        deal_words(1)
+        deal_scales(1)
 
         def first_product(i, t, tag):
             acc = psum.tile([P, S], F32, name=tag, tag=tag)
@@ -120,9 +133,9 @@ def tile_picked_yfirefr_new_p_kernel(
         fu = [first_product(1, t, "bank%d" % (PACK + t)) for t in range(PACK)]
         wd.extend([first_product(0, t, "bank%d" % t) for t in range(2, PACK)])
 
-        burn5 = keep.tile([P, PACK, S], F32, name="burn5")
-        for t in range(PACK):
-            nc.vector.tensor_scalar(burn5[:, t, :], burn[t][:, :S], 5.0, -5.0, ALU.mult, ALU.add)
+        for t in range(2, PACK):
+            nc.gpsimd.memset(burn[t][:, S:], 0.0)
+            nc.vector.tensor_scalar(burn[t][:, :S], th[:, t, :], 0.5, 0.5, ALU.mult, ALU.add)
         gain = keep.tile([P, PACK], F32, name="gain")
         nc.vector.tensor_scalar(gain[:], unit_t[:], -0.2, None, ALU.mult)
 
@@ -135,7 +148,10 @@ def tile_picked_yfirefr_new_p_kernel(
             nc.scalar.activation(tw[:, t, :], wd[t][:], ACT.Tanh)
             nc.scalar.activation(wind2[:, t, :], tw[:, t, :], ACT.Exp, bias=math.log(2.0), scale=0.9)
             nc.vector.tensor_tensor(upwind[:, t, :], burn[t][:].indirect(uw_t[:]), wind2[:, t, :], ALU.mult)
-            nc.vector.tensor_tensor(heat2[:, t, :], burn[t][:].indirect(sd_t[:]), upwind[:, t, :], ALU.add)
+            if t < 2:
+                nc.vector.tensor_tensor(heat2[:, t, :], upwind[:, t, :], side[t][:], ALU.add)
+            else:
+                nc.vector.tensor_tensor(heat2[:, t, :], burn[t][:].indirect(sd_t[:]), upwind[:, t, :], ALU.add)
 
         efu = keep.tile([P, PACK, S], F32, name="efu")
         efu_c = keep.tile([P, PACK, S], F32, name="efu_c")
@@ -143,7 +159,7 @@ def tile_picked_yfirefr_new_p_kernel(
         fuel = keep.tile([P, PACK, S], F32, name="fuel")
         log_heat = keep.tile([P, PACK, S], F32, name="log_heat")
         log_fuel = keep.tile([P, PACK, S], F32, name="log_fuel")
-        fb = keep.tile([P, PACK, HALF], F32, name="fb")
+        fb = keep.tile([P, PACK, 384], F32, name="fb")
         heat_rows(0)
         heat_rows(1)
         for t in range(PACK):
@@ -152,18 +168,21 @@ def tile_picked_yfirefr_new_p_kernel(
         heat_rows(2)
         heat_rows(3)
         for t in range(PACK):
-            nc.scalar.activation(soft[:, t, :], efu_c[:, t, :], ACT.Ln, bias=math.exp(0.1), scale=math.exp(0.1))
-            nc.vector.scalar_tensor_tensor(fuel[:, t, :], fu[t][:], 0.1, soft[:, t, :], ALU.add, ALU.max)
+            nc.scalar.activation(soft[:, t, :], efu_c[:, t, :], ACT.Ln, bias=math.exp(2.6), scale=math.exp(2.6))
+            nc.vector.scalar_tensor_tensor(fuel[:, t, :], fu[t][:], 2.6, soft[:, t, :], ALU.add, ALU.max)
         for t in range(PACK):
             nc.scalar.activation(log_heat[:, t, :], heat2[:, t, :], ACT.Ln, bias=TINY, scale=0.15)
         for t in range(PACK):
-            nc.scalar.activation(log_fuel[:, t, :], fuel[:, t, :], ACT.Ln)
+            nc.scalar.activation(log_fuel[:, t, :], fuel[:, t, :], ACT.Ln, bias=-2.5)
         for t in range(PACK):
-            nc.vector.tensor_copy(fb[:, t, :], fuel[:, t, :].indirect(uw_t[:, : HALF // 16]))
+            nc.vector.tensor_copy(fb[:, t, :HALF], fuel[:, t, :].indirect(uw_t[:, : HALF // 16]))
 
         logit = keep.tile([P, PACK, S], F32, name="logit")
         for lo, hi in CHUNKS:
             nc.vector.tensor_tensor(logit[:, :, lo:hi], log_heat[:, :, lo:hi], log_fuel[:, :, lo:hi], ALU.subtract)
+
+        for t in range(PACK):
+            nc.vector.tensor_copy(fb[:, t, HALF:], fuel[:, t, :].indirect(uw_t[:, HALF // 16 : 384 // 16]))
 
         out_rows = out.rearrange("(a p) s -> p a s", p=P)
         tzs = []
@@ -171,6 +190,9 @@ def tile_picked_yfirefr_new_p_kernel(
             w = hi - lo
             tz = keep.tile([P, PACK, w], F32, name="tz%d" % c)
             tzs.append(tz)
+            if c == 3:
+                for t in range(PACK):
+                    nc.scalar.activation(tzs[1][:, t, :], fuel[:, t, :].indirect(uw_t[:, lo // 16 : hi // 16]), ACT.Copy)
             miss5 = keep.tile([P, PACK, w], F32, name="miss5_%d" % c)
             short5 = keep.tile([P, PACK, w], F32, name="short5_%d" % c)
             total = keep.tile([P, PACK, w], F32, name="total%d" % c)
@@ -178,14 +200,11 @@ def tile_picked_yfirefr_new_p_kernel(
             codes = keep.tile([P, w], U32, name="codes%d" % c, align_bytes=64)
             scales = keep.tile([P, w], U8, name="scales%d" % c, align_bytes=64)
             res = keep.tile([P, N // P, w], F32, name="res%d" % c)
-            if lo >= HALF:
-                for t in range(PACK):
-                    nc.scalar.activation(tzs[c - 2][:, t, :], fuel[:, t, :].indirect(uw_t[:, lo // 16 : hi // 16]), ACT.Copy)
             nc.scalar.activation(tz[:], logit[:, :, lo:hi], ACT.Tanh, scale=0.5)
             nc.scalar.activation(miss5[:], tz[:], ACT.Exp, bias=math.log(5.0) - 0.5 / 0.3, scale=-0.5 / 0.3)
-            nc.vector.tensor_tensor(short5[:], miss5[:], burn5[:, :, lo:hi], ALU.add)
-            fb_c = tzs[c - 2][:] if lo >= HALF else fb[:, :, lo:hi]
-            nc.vector.scalar_tensor_tensor(total[:], short5[:], 0.0, fb_c, ALU.min, ALU.subtract)
+            nc.vector.scalar_tensor_tensor(short5[:], th[:, :, lo:hi], 2.5, miss5[:], ALU.mult, ALU.add)
+            fb_c = tzs[1][:] if c == 3 else fb[:, :, lo:hi]
+            nc.vector.scalar_tensor_tensor(total[:], short5[:], 2.5, fb_c, ALU.min, ALU.subtract)
             nc.vector.tensor_tensor(
                 hid[:].rearrange("p (c i) t -> p c t i", i=4),
                 total[:].rearrange("p t (c i) -> p c t i", i=4),

@@ -47,36 +47,33 @@ def tile_picked_yfirefr_new_p_kernel(
         xw = reuse.tile([P, T], I32, name="xw", offset=0, align_bytes=64)
         xs = keep.tile([P, T], U8, name="xs", align_bytes=64)
         w_raw = [keep.tile([P, 2 * H], U8, name="w_raw%d" % i, align_bytes=64) for i in range(2)]
-        ws_raw = [keep.tile([P, H], U8, name="ws_raw%d" % i, align_bytes=64) for i in range(2)]
+        ws_raw = [keep.tile([P, H], U8, name="ws_raw%d" % i, tag="ws_raw%d" % i, align_bytes=64) for i in range(2)]
         w3w = keep.tile([P, 2 * N], U8, name="w3w", align_bytes=64)
         w3s = keep.tile([P, N], U8, name="w3s", align_bytes=64)
         ign_t = keep.tile([P, PACK, S], F32, name="ign_t")
         unit_t = keep.tile([P, PACK], F32, name="unit_t")
-        burn = [keep.tile([P, S + SPARE], F32, name="burn%d" % t) for t in range(2)]
-        burn.extend(
-            [reuse.tile([P, S + SPARE], F32, name="burn%d" % t, offset=H + (t - 2) * 2112, align_bytes=64) for t in range(2, PACK)]
-        )
+        burn = [keep.tile([P, S + SPARE], F32, name="burn%d" % t) for t in range(PACK)]
 
         nc.gpsimd.memset(xs[:].bitcast(I32), 0)
         nc.vector.memset(ws_raw[0][:].bitcast(I32), 0)
         nc.vector.memset(ws_raw[1][:].bitcast(I32), 0)
         nc.vector.memset(w3s[:].bitcast(I32), 0)
-        for t in range(2):
+        for t in range(PACK):
             nc.vector.memset(burn[t][:, S:], 0.0)
 
         nc.sync.dma_start(offs_t[:], offs)
-        nc.sync.dma_start(sd_t[:], sd)
         nc.sync.dma_start(out=w_raw[0][:], in_=w2_words[0])
+        nc.sync.dma_start(sd_t[:], sd)
+        nc.sync.dma_start(uw_t[:], uw)
+        nc.sync.dma_start(out=unit_t[:], in_=unit.rearrange("(p t) o -> p (t o)", t=PACK))
+        nc.sync.dma_start(out=w_raw[1][:], in_=w1_words[0])
+        nc.sync.dma_start(out=w3w[:], in_=w3_words[0])
         nc.sync.dma_start(out=ign_t[:], in_=ign.rearrange("(p t) s -> p t s", t=PACK))
         load_scale_rows(xs, x_scales, range(4))
         load_scale_rows(ws_raw[0], w2_scales, range(2))
         nc.sync.dma_start(out=xw[:], in_=x_words[0].rearrange("p n t -> p (n t)").bitcast(I32))
         load_scale_rows(ws_raw[0], w2_scales, range(2, 4))
-        nc.sync.dma_start(out=w_raw[1][:], in_=w1_words[0])
         load_scale_rows(ws_raw[1], w1_scales, range(4))
-        nc.sync.dma_start(uw_t[:], uw)
-        nc.sync.dma_start(out=unit_t[:], in_=unit.rearrange("(p t) o -> p (t o)", t=PACK))
-        nc.sync.dma_start(out=w3w[:], in_=w3_words[0])
         load_scale_rows(w3s, w3_scales, range(4))
 
         th = keep.tile([P, PACK, S], F32, name="th")
@@ -88,10 +85,7 @@ def tile_picked_yfirefr_new_p_kernel(
             nc.scalar.activation(side[t][:], th_flat[:, S * t : S * (t + 2)].indirect(sd_t[:]), ACT.Copy, bias=0.5, scale=0.5)
 
         w_dealt = [keep.tile([P, 2 * H], U8, name="w_dealt%d" % i, align_bytes=64) for i in range(2)]
-        ws_dealt = [
-            keep.tile([P, H], U8, name="ws_dealt0", align_bytes=64),
-            reuse.tile([P, H], U8, name="ws_dealt1", offset=0, align_bytes=64),
-        ]
+        ws_dealt = {}
         xg_w = keep.tile([P, S], U32, name="xg_w", align_bytes=64)
         xg_s = keep.tile([P, S], U8, name="xg_s", align_bytes=64)
 
@@ -101,27 +95,30 @@ def tile_picked_yfirefr_new_p_kernel(
                 in_=w_raw[i][:].rearrange("p (m t b) -> p m t b", t=PACK, b=2),
             )
 
-        def deal_scales(i):
+        def deal_scales(i, first, count, dealt):
             nc.vector.tensor_copy(
-                out=ws_dealt[i][:].rearrange("p (t m) -> p m t", t=PACK),
-                in_=ws_raw[i][:].rearrange("p (m t) -> p m t", t=PACK),
+                out=dealt[:].rearrange("p t m -> p m t"),
+                in_=ws_raw[i][:].rearrange("p (m t) -> p m t", t=PACK)[:, :, first : first + count],
             )
+            for t in range(count):
+                ws_dealt.setdefault((i, first + t), dealt[:, t, :])
 
         deal_words(0)
         nc.vector.tensor_copy(xg_s[:], xs[:].indirect(offs_t[:]))
         for t in range(2):
             nc.vector.tensor_scalar(burn[t][:, :S], th[:, t, :], 0.5, 0.5, ALU.mult, ALU.add)
-        deal_scales(0)
-        nc.vector.tensor_copy(xg_w[:], xw[:].bitcast(U32).indirect(offs_t[:]))
         deal_words(1)
-        deal_scales(1)
+        nc.vector.tensor_copy(xg_w[:], xw[:].bitcast(U32).indirect(offs_t[:]))
+        deal_scales(0, 0, 2, keep.tile([P, 2, P], U8, name="w2s_first", align_bytes=64))
+        deal_scales(1, 0, PACK, reuse.tile([P, PACK, P], U8, name="w1s_dealt", offset=0, align_bytes=64))
+        deal_scales(0, 2, 2, keep.tile([P, 2, P], U8, name="w2s_last", tag="ws_raw1", align_bytes=64))
 
         def first_product(i, t, tag):
             acc = psum.tile([P, S], F32, name=tag, tag=tag)
             nc.tensor.matmul_mx(
                 out=acc[:],
                 lhsT=w_dealt[i][:, 2 * P * t : 2 * P * (t + 1)].bitcast(FP4X4),
-                lhsT_scale=ws_dealt[i][:, P * t : P * (t + 1)],
+                lhsT_scale=ws_dealt[(i, t)],
                 rhs=xg_w[:].bitcast(FP8X4),
                 rhs_scale=xg_s[:],
                 start=True,
@@ -134,13 +131,12 @@ def tile_picked_yfirefr_new_p_kernel(
         wd.extend([first_product(0, t, "bank%d" % t) for t in range(2, PACK)])
 
         for t in range(2, PACK):
-            nc.gpsimd.memset(burn[t][:, S:], 0.0)
-            nc.vector.tensor_scalar(burn[t][:, :S], th[:, t, :], 0.5, 0.5, ALU.mult, ALU.add)
+            nc.gpsimd.tensor_scalar(burn[t][:, :S], th[:, t, :], 0.5, 0.5, ALU.mult, ALU.add)
         gain = keep.tile([P, PACK], F32, name="gain")
         nc.vector.tensor_scalar(gain[:], unit_t[:], -0.2, None, ALU.mult)
 
-        tw = keep.tile([P, PACK, S], F32, name="tw")
-        wind2 = keep.tile([P, PACK, S], F32, name="wind2")
+        tw = keep.tile([P, PACK, S], F32, name="tw", tag="tw")
+        wind2 = keep.tile([P, PACK, S], F32, name="wind2", tag="wind2")
         upwind = keep.tile([P, PACK, S], F32, name="upwind")
         heat2 = keep.tile([P, PACK, S], F32, name="heat2")
 
@@ -155,9 +151,7 @@ def tile_picked_yfirefr_new_p_kernel(
 
         efu = keep.tile([P, PACK, S], F32, name="efu")
         efu_c = keep.tile([P, PACK, S], F32, name="efu_c")
-        soft = keep.tile([P, PACK, S], F32, name="soft")
         fuel = keep.tile([P, PACK, S], F32, name="fuel")
-        log_heat = keep.tile([P, PACK, S], F32, name="log_heat")
         log_fuel = keep.tile([P, PACK, S], F32, name="log_fuel")
         fb = keep.tile([P, PACK, 384], F32, name="fb")
         heat_rows(0)
@@ -167,6 +161,8 @@ def tile_picked_yfirefr_new_p_kernel(
         nc.vector.tensor_scalar(efu_c[:], efu[:], HUGE, None, ALU.min)
         heat_rows(2)
         heat_rows(3)
+        soft = keep.tile([P, PACK, S], F32, name="soft", tag="tw")
+        log_heat = keep.tile([P, PACK, S], F32, name="log_heat", tag="wind2")
         for t in range(PACK):
             nc.scalar.activation(soft[:, t, :], efu_c[:, t, :], ACT.Ln, bias=math.exp(2.6), scale=math.exp(2.6))
             nc.vector.scalar_tensor_tensor(fuel[:, t, :], fu[t][:], 2.6, soft[:, t, :], ALU.add, ALU.max)
@@ -175,14 +171,11 @@ def tile_picked_yfirefr_new_p_kernel(
         for t in range(PACK):
             nc.scalar.activation(log_fuel[:, t, :], fuel[:, t, :], ACT.Ln, bias=-2.5)
         for t in range(PACK):
-            nc.vector.tensor_copy(fb[:, t, :HALF], fuel[:, t, :].indirect(uw_t[:, : HALF // 16]))
+            nc.vector.tensor_copy(fb[:, t, :], fuel[:, t, :].indirect(uw_t[:, : 384 // 16]))
 
         logit = keep.tile([P, PACK, S], F32, name="logit")
-        for lo, hi in CHUNKS:
+        for lo, hi in ((0, 128), (128, S)):
             nc.vector.tensor_tensor(logit[:, :, lo:hi], log_heat[:, :, lo:hi], log_fuel[:, :, lo:hi], ALU.subtract)
-
-        for t in range(PACK):
-            nc.vector.tensor_copy(fb[:, t, HALF:], fuel[:, t, :].indirect(uw_t[:, HALF // 16 : 384 // 16]))
 
         out_rows = out.rearrange("(a p) s -> p a s", p=P)
         tzs = []

@@ -18,10 +18,18 @@ ALU = mybir.AluOpType
 ACT = mybir.ActivationFunctionType
 
 P = 128
-PACK = 4
+PLANES = 4
+QUADRANTS = 4
+PER_COLUMN = 16
+WIND, FUEL = 0, 1
+
 SPARE = 8
-HALF = S // 2
-CHUNKS = ((0, 128), (128, 256), (256, 384), (384, 512))
+CHUNK = 128
+CHUNKS = S // CHUNK
+LEAD = CHUNK // 2
+SIDE_PLANES_ON_SCALAR = 3
+FUEL_CELLS_ON_VECTOR = S - CHUNK
+
 TINY = 2.0 ** -60
 HUGE = 2.0 ** 60
 
@@ -33,188 +41,227 @@ def tile_picked_yfirefr_new_p_kernel(
     with ExitStack() as ctx:
         keep = ctx.enter_context(tc.tile_pool(name="keep", bufs=1))
         psum = ctx.enter_context(tc.psum_pool(name="psum", bufs=1))
-
         reuse = ctx.enter_context(tc.tile_pool(name="reuse", bufs=1))
 
-        def load_scale_rows(plane, rows, quadrants):
+        def load_scale_rows(scale_tile, rows, quadrants):
             for q in quadrants:
-                nc.sync.dma_start(out=plane[32 * q : 32 * q + 4, :].bitcast(I32), in_=rows[0, 4 * q : 4 * q + 4, :].bitcast(I32))
+                nc.sync.dma_start(
+                    out=scale_tile[32 * q : 32 * q + 4, :].bitcast(I32), in_=rows[0, 4 * q : 4 * q + 4, :].bitcast(I32)
+                )
 
-        offs_t = keep.tile([P, S // 16], U16, name="offs_t")
-        uw_t = keep.tile([P, S // 16], U16, name="uw_t")
-        sd_t = keep.tile([P, S // 16], U16, name="sd_t")
+        offs_list = keep.tile([P, S // PER_COLUMN], U16, name="offs_list")
+        uw_list = keep.tile([P, S // PER_COLUMN], U16, name="uw_list")
+        sd_list = keep.tile([P, S // PER_COLUMN], U16, name="sd_list")
 
-        xw = reuse.tile([P, T], I32, name="xw", offset=0, align_bytes=64)
-        xs = keep.tile([P, T], U8, name="xs", align_bytes=64)
-        w_raw = [keep.tile([P, 2 * H], U8, name="w_raw%d" % i, align_bytes=64) for i in range(2)]
-        ws_raw = [keep.tile([P, H], U8, name="ws_raw%d" % i, tag="ws_raw%d" % i, align_bytes=64) for i in range(2)]
-        w3w = keep.tile([P, 2 * N], U8, name="w3w", align_bytes=64)
-        w3s = keep.tile([P, N], U8, name="w3s", align_bytes=64)
-        ign_t = keep.tile([P, PACK, S], F32, name="ign_t")
-        unit_t = keep.tile([P, PACK], F32, name="unit_t")
-        burn = [keep.tile([P, S + SPARE], F32, name="burn%d" % t) for t in range(PACK)]
+        x_word_table = reuse.tile([P, T], I32, name="x_word_table", offset=0, align_bytes=64)
+        x_scale_table = keep.tile([P, T], U8, name="x_scale_table", align_bytes=64)
+        w_words = [keep.tile([P, 2 * H], U8, name="w_words%d" % i, align_bytes=64) for i in (WIND, FUEL)]
+        w_scales = [
+            keep.tile([P, H], U8, name="w_scales%d" % i, tag="w_scales%d" % i, align_bytes=64) for i in (WIND, FUEL)
+        ]
+        w3_word_tile = keep.tile([P, 2 * N], U8, name="w3_word_tile", align_bytes=64)
+        w3_scale_tile = keep.tile([P, N], U8, name="w3_scale_tile", align_bytes=64)
+        ign_pair = [keep.tile([P, 2, S], F32, name="ign_pair%d" % i) for i in range(2)]
+        unit_tile = keep.tile([P, PLANES], F32, name="unit_tile")
+        burn = [keep.tile([P, S + SPARE], F32, name="burn%d" % t) for t in range(PLANES)]
 
-        nc.gpsimd.memset(xs[:].bitcast(I32), 0)
-        nc.vector.memset(ws_raw[0][:].bitcast(I32), 0)
-        nc.vector.memset(ws_raw[1][:].bitcast(I32), 0)
-        nc.vector.memset(w3s[:].bitcast(I32), 0)
-        for t in range(PACK):
+        nc.gpsimd.memset(x_scale_table[:].bitcast(I32), 0)
+        nc.vector.memset(w_scales[WIND][:].bitcast(I32), 0)
+        nc.vector.memset(w_scales[FUEL][:].bitcast(I32), 0)
+        nc.vector.memset(w3_scale_tile[:].bitcast(I32), 0)
+        for t in range(PLANES):
             nc.vector.memset(burn[t][:, S:], 0.0)
 
-        nc.sync.dma_start(offs_t[:], offs)
-        nc.sync.dma_start(out=w_raw[0][:], in_=w2_words[0])
-        nc.sync.dma_start(sd_t[:], sd)
-        nc.sync.dma_start(uw_t[:], uw)
-        nc.sync.dma_start(out=unit_t[:], in_=unit.rearrange("(p t) o -> p (t o)", t=PACK))
-        nc.sync.dma_start(out=w_raw[1][:], in_=w1_words[0])
-        nc.sync.dma_start(out=w3w[:], in_=w3_words[0])
-        nc.sync.dma_start(out=ign_t[:], in_=ign.rearrange("(p t) s -> p t s", t=PACK))
-        load_scale_rows(xs, x_scales, range(4))
-        load_scale_rows(ws_raw[0], w2_scales, range(2))
-        nc.sync.dma_start(out=xw[:], in_=x_words[0].rearrange("p n t -> p (n t)").bitcast(I32))
-        load_scale_rows(ws_raw[0], w2_scales, range(2, 4))
-        load_scale_rows(ws_raw[1], w1_scales, range(4))
-        load_scale_rows(w3s, w3_scales, range(4))
+        ign_planes = ign.rearrange("(p t) s -> p t s", t=PLANES)
+        nc.sync.dma_start(offs_list[:], offs)
+        nc.sync.dma_start(out=w_words[WIND][:], in_=w2_words[0])
+        nc.sync.dma_start(sd_list[:], sd)
+        nc.sync.dma_start(uw_list[:], uw)
+        nc.sync.dma_start(out=unit_tile[:], in_=unit.rearrange("(p t) o -> p (t o)", t=PLANES))
+        nc.sync.dma_start(out=w_words[FUEL][:], in_=w1_words[0])
+        nc.sync.dma_start(out=ign_pair[0][:], in_=ign_planes[:, 0:2, :])
+        nc.sync.dma_start(out=ign_pair[1][:], in_=ign_planes[:, 2:4, :])
+        load_scale_rows(x_scale_table, x_scales, range(QUADRANTS))
+        load_scale_rows(w_scales[WIND], w2_scales, range(1))
+        nc.sync.dma_start(out=x_word_table[:], in_=x_words[0].rearrange("p n t -> p (n t)").bitcast(I32))
+        load_scale_rows(w_scales[WIND], w2_scales, range(1, QUADRANTS))
+        load_scale_rows(w_scales[FUEL], w1_scales, range(QUADRANTS))
+        nc.sync.dma_start(out=w3_word_tile[:], in_=w3_words[0])
+        load_scale_rows(w3_scale_tile, w3_scales, range(QUADRANTS))
 
-        th = keep.tile([P, PACK, S], F32, name="th")
+        th = keep.tile([P, PLANES, S], F32, name="th")
         th_flat = th[:].rearrange("p t s -> p (t s)")
-        side = [keep.tile([P, S], F32, name="side%d" % t) for t in range(2)]
+        side = [keep.tile([P, S], F32, name="side%d" % t) for t in range(SIDE_PLANES_ON_SCALAR)]
         for i in range(2):
-            nc.scalar.activation(th[:, 2 * i : 2 * i + 2, :], ign_t[:, 2 * i : 2 * i + 2, :], ACT.Tanh, scale=0.5)
-        for t in range(2):
-            nc.scalar.activation(side[t][:], th_flat[:, S * t : S * (t + 2)].indirect(sd_t[:]), ACT.Copy, bias=0.5, scale=0.5)
+            nc.scalar.activation(th[:, 2 * i : 2 * i + 2, :], ign_pair[i][:], ACT.Tanh, scale=0.5)
+        for t in range(SIDE_PLANES_ON_SCALAR):
+            window = th_flat[:, S * t : S * (t + 2)]
+            nc.scalar.activation(side[t][:], window.indirect(sd_list[:]), ACT.Copy, bias=0.5, scale=0.5)
 
-        w_dealt = [keep.tile([P, 2 * H], U8, name="w_dealt%d" % i, align_bytes=64) for i in range(2)]
-        ws_dealt = {}
-        xg_w = keep.tile([P, S], U32, name="xg_w", align_bytes=64)
-        xg_s = keep.tile([P, S], U8, name="xg_s", align_bytes=64)
+        dealt_words = [keep.tile([P, 2 * H], U8, name="dealt_words%d" % i, align_bytes=64) for i in (WIND, FUEL)]
+        dealt_scales = {}
+        cell_words = keep.tile([P, S], U32, name="cell_words", align_bytes=64)
+        cell_scales = keep.tile([P, S], U8, name="cell_scales", align_bytes=64)
 
         def deal_words(i):
             nc.vector.tensor_copy(
-                out=w_dealt[i][:].rearrange("p (t m b) -> p m t b", t=PACK, b=2),
-                in_=w_raw[i][:].rearrange("p (m t b) -> p m t b", t=PACK, b=2),
+                out=dealt_words[i][:].rearrange("p (t m b) -> p m t b", t=PLANES, b=2),
+                in_=w_words[i][:].rearrange("p (m t b) -> p m t b", t=PLANES, b=2),
             )
 
         def deal_scales(i, first, count, dealt):
             nc.vector.tensor_copy(
                 out=dealt[:].rearrange("p t m -> p m t"),
-                in_=ws_raw[i][:].rearrange("p (m t) -> p m t", t=PACK)[:, :, first : first + count],
+                in_=w_scales[i][:].rearrange("p (m t) -> p m t", t=PLANES)[:, :, first : first + count],
             )
             for t in range(count):
-                ws_dealt.setdefault((i, first + t), dealt[:, t, :])
+                dealt_scales.setdefault((i, first + t), dealt[:, t, :])
 
-        deal_words(0)
-        nc.vector.tensor_copy(xg_s[:], xs[:].indirect(offs_t[:]))
-        for t in range(2):
+        deal_words(WIND)
+        nc.vector.tensor_copy(cell_scales[:], x_scale_table[:].indirect(offs_list[:]))
+        for t in range(PLANES):
             nc.vector.tensor_scalar(burn[t][:, :S], th[:, t, :], 0.5, 0.5, ALU.mult, ALU.add)
-        deal_words(1)
-        nc.vector.tensor_copy(xg_w[:], xw[:].bitcast(U32).indirect(offs_t[:]))
-        deal_scales(0, 0, 2, keep.tile([P, 2, P], U8, name="w2s_first", align_bytes=64))
-        deal_scales(1, 0, PACK, reuse.tile([P, PACK, P], U8, name="w1s_dealt", offset=0, align_bytes=64))
-        deal_scales(0, 2, 2, keep.tile([P, 2, P], U8, name="w2s_last", tag="ws_raw1", align_bytes=64))
+        deal_words(FUEL)
+        nc.vector.tensor_copy(cell_words[:], x_word_table[:].bitcast(U32).indirect(offs_list[:]))
+        deal_scales(WIND, 0, 2, keep.tile([P, 2, P], U8, name="wind_scales_first", align_bytes=64))
+        deal_scales(FUEL, 0, PLANES, reuse.tile([P, PLANES, P], U8, name="fuel_scales", offset=0, align_bytes=64))
+        deal_scales(
+            WIND, 2, 2, keep.tile([P, 2, P], U8, name="wind_scales_last", tag="w_scales%d" % FUEL, align_bytes=64)
+        )
 
-        def first_product(i, t, tag):
-            acc = psum.tile([P, S], F32, name=tag, tag=tag)
+        def first_product(i, t):
+            bank = "bank%d" % (PLANES * i + t)
+            acc = psum.tile([P, S], F32, name=bank, tag=bank)
             nc.tensor.matmul_mx(
                 out=acc[:],
-                lhsT=w_dealt[i][:, 2 * P * t : 2 * P * (t + 1)].bitcast(FP4X4),
-                lhsT_scale=ws_dealt[(i, t)],
-                rhs=xg_w[:].bitcast(FP8X4),
-                rhs_scale=xg_s[:],
+                lhsT=dealt_words[i][:, 2 * P * t : 2 * P * (t + 1)].bitcast(FP4X4),
+                lhsT_scale=dealt_scales[(i, t)],
+                rhs=cell_words[:].bitcast(FP8X4),
+                rhs_scale=cell_scales[:],
                 start=True,
                 stop=True,
             )
             return acc
 
-        wd = [first_product(0, t, "bank%d" % t) for t in range(2)]
-        fu = [first_product(1, t, "bank%d" % (PACK + t)) for t in range(PACK)]
-        wd.extend([first_product(0, t, "bank%d" % t) for t in range(2, PACK)])
+        wd = [first_product(WIND, t) for t in range(2)]
+        fu = [first_product(FUEL, t) for t in range(PLANES)]
+        wd.extend([first_product(WIND, t) for t in range(2, PLANES)])
 
-        for t in range(2, PACK):
-            nc.gpsimd.tensor_scalar(burn[t][:, :S], th[:, t, :], 0.5, 0.5, ALU.mult, ALU.add)
-        gain = keep.tile([P, PACK], F32, name="gain")
-        nc.vector.tensor_scalar(gain[:], unit_t[:], -0.2, None, ALU.mult)
+        gain = keep.tile([P, PLANES], F32, name="gain")
+        nc.vector.tensor_scalar(gain[:], unit_tile[:], -0.2, None, ALU.mult)
 
-        tw = keep.tile([P, PACK, S], F32, name="tw", tag="tw")
-        wind2 = keep.tile([P, PACK, S], F32, name="wind2", tag="wind2")
-        upwind = keep.tile([P, PACK, S], F32, name="upwind")
-        heat2 = keep.tile([P, PACK, S], F32, name="heat2")
+        tanh_wd = keep.tile([P, PLANES, S], F32, name="tanh_wd", tag="tanh_wd")
+        wind2 = keep.tile([P, PLANES, S], F32, name="wind2", tag="wind2")
+        upwind = keep.tile([P, PLANES, S], F32, name="upwind")
+        heat2 = keep.tile([P, PLANES, S], F32, name="heat2")
 
-        def heat_rows(t):
-            nc.scalar.activation(tw[:, t, :], wd[t][:], ACT.Tanh)
-            nc.scalar.activation(wind2[:, t, :], tw[:, t, :], ACT.Exp, bias=math.log(2.0), scale=0.9)
-            nc.vector.tensor_tensor(upwind[:, t, :], burn[t][:].indirect(uw_t[:]), wind2[:, t, :], ALU.mult)
-            if t < 2:
+        def heat_plane(t):
+            nc.scalar.activation(tanh_wd[:, t, :], wd[t][:], ACT.Tanh)
+            nc.scalar.activation(wind2[:, t, :], tanh_wd[:, t, :], ACT.Exp, bias=math.log(2.0), scale=0.9)
+            nc.vector.tensor_tensor(upwind[:, t, :], burn[t][:].indirect(uw_list[:]), wind2[:, t, :], ALU.mult)
+            if t < SIDE_PLANES_ON_SCALAR:
                 nc.vector.tensor_tensor(heat2[:, t, :], upwind[:, t, :], side[t][:], ALU.add)
             else:
-                nc.vector.tensor_tensor(heat2[:, t, :], burn[t][:].indirect(sd_t[:]), upwind[:, t, :], ALU.add)
+                nc.vector.tensor_tensor(heat2[:, t, :], burn[t][:].indirect(sd_list[:]), upwind[:, t, :], ALU.add)
 
-        efu = keep.tile([P, PACK, S], F32, name="efu")
-        efu_c = keep.tile([P, PACK, S], F32, name="efu_c")
-        fuel = keep.tile([P, PACK, S], F32, name="fuel")
-        log_fuel = keep.tile([P, PACK, S], F32, name="log_fuel")
-        fb = keep.tile([P, PACK, 384], F32, name="fb")
-        heat_rows(0)
-        heat_rows(1)
-        for t in range(PACK):
-            nc.scalar.activation(efu[:, t, :], fu[t][:], ACT.Exp)
-        nc.vector.tensor_scalar(efu_c[:], efu[:], HUGE, None, ALU.min)
-        heat_rows(2)
-        heat_rows(3)
-        soft = keep.tile([P, PACK, S], F32, name="soft", tag="tw")
-        log_heat = keep.tile([P, PACK, S], F32, name="log_heat", tag="wind2")
-        for t in range(PACK):
-            nc.scalar.activation(soft[:, t, :], efu_c[:, t, :], ACT.Ln, bias=math.exp(2.6), scale=math.exp(2.6))
-            nc.vector.scalar_tensor_tensor(fuel[:, t, :], fu[t][:], 2.6, soft[:, t, :], ALU.add, ALU.max)
-        for t in range(PACK):
+        exp_fu = keep.tile([P, PLANES, S], F32, name="exp_fu")
+        exp_fu_bounded = keep.tile([P, PLANES, S], F32, name="exp_fu_bounded")
+        fuel_plus = keep.tile([P, PLANES, S], F32, name="fuel_plus")
+        log_fuel = keep.tile([P, PLANES, S], F32, name="log_fuel")
+        fuel_up = keep.tile([P, PLANES, FUEL_CELLS_ON_VECTOR], F32, name="fuel_up")
+
+        heat_plane(0)
+        heat_plane(1)
+        for t in range(PLANES):
+            nc.scalar.activation(exp_fu[:, t, :], fu[t][:], ACT.Exp)
+        nc.vector.tensor_scalar(exp_fu_bounded[:], exp_fu[:], HUGE, None, ALU.min)
+        heat_plane(2)
+        heat_plane(3)
+
+        soft_plus = keep.tile([P, PLANES, S], F32, name="soft_plus", tag="tanh_wd")
+        log_heat = keep.tile([P, PLANES, S], F32, name="log_heat", tag="wind2")
+        for t in range(PLANES):
+            nc.scalar.activation(
+                soft_plus[:, t, :], exp_fu_bounded[:, t, :], ACT.Ln, bias=math.exp(2.6), scale=math.exp(2.6)
+            )
+            nc.vector.scalar_tensor_tensor(fuel_plus[:, t, :], fu[t][:], 2.6, soft_plus[:, t, :], ALU.add, ALU.max)
+        for t in range(PLANES):
             nc.scalar.activation(log_heat[:, t, :], heat2[:, t, :], ACT.Ln, bias=TINY, scale=0.15)
-        for t in range(PACK):
-            nc.scalar.activation(log_fuel[:, t, :], fuel[:, t, :], ACT.Ln, bias=-2.5)
-        for t in range(PACK):
-            nc.vector.tensor_copy(fb[:, t, :], fuel[:, t, :].indirect(uw_t[:, : 384 // 16]))
+        for t in range(PLANES):
+            nc.scalar.activation(log_fuel[:, t, :], fuel_plus[:, t, :], ACT.Ln, bias=-2.5)
+        for t in range(PLANES):
+            entries = uw_list[:, : FUEL_CELLS_ON_VECTOR // PER_COLUMN]
+            nc.vector.tensor_copy(fuel_up[:, t, :], fuel_plus[:, t, :].indirect(entries))
 
-        logit = keep.tile([P, PACK, S], F32, name="logit")
-        for lo, hi in ((0, 128), (128, S)):
+        logit = keep.tile([P, PLANES, S], F32, name="logit")
+        for lo, hi in ((0, LEAD), (LEAD, S // 2), (S // 2, S)):
             nc.vector.tensor_tensor(logit[:, :, lo:hi], log_heat[:, :, lo:hi], log_fuel[:, :, lo:hi], ALU.subtract)
 
         out_rows = out.rearrange("(a p) s -> p a s", p=P)
-        tzs = []
-        for c, (lo, hi) in enumerate(CHUNKS):
-            w = hi - lo
-            tz = keep.tile([P, PACK, w], F32, name="tz%d" % c)
-            tzs.append(tz)
-            if c == 3:
-                for t in range(PACK):
-                    nc.scalar.activation(tzs[1][:, t, :], fuel[:, t, :].indirect(uw_t[:, lo // 16 : hi // 16]), ACT.Copy)
-            miss5 = keep.tile([P, PACK, w], F32, name="miss5_%d" % c)
-            short5 = keep.tile([P, PACK, w], F32, name="short5_%d" % c)
-            total = keep.tile([P, PACK, w], F32, name="total%d" % c)
-            hid = keep.tile([P, w, PACK], BF16, name="hid%d" % c, align_bytes=64)
-            codes = keep.tile([P, w], U32, name="codes%d" % c, align_bytes=64)
-            scales = keep.tile([P, w], U8, name="scales%d" % c, align_bytes=64)
-            res = keep.tile([P, N // P, w], F32, name="res%d" % c)
-            nc.scalar.activation(tz[:], logit[:, :, lo:hi], ACT.Tanh, scale=0.5)
-            nc.scalar.activation(miss5[:], tz[:], ACT.Exp, bias=math.log(5.0) - 0.5 / 0.3, scale=-0.5 / 0.3)
-            nc.vector.scalar_tensor_tensor(short5[:], th[:, :, lo:hi], 2.5, miss5[:], ALU.mult, ALU.add)
-            fb_c = tzs[1][:] if c == 3 else fb[:, :, lo:hi]
-            nc.vector.scalar_tensor_tensor(total[:], short5[:], 2.5, fb_c, ALU.min, ALU.subtract)
+        tanh_logit = []
+        for c in range(CHUNKS):
+            lo = c * CHUNK
+            tanh_logit.append(keep.tile([P, PLANES, CHUNK], F32, name="tanh_logit%d" % c))
+            if lo < FUEL_CELLS_ON_VECTOR:
+                fuel_up_chunk = fuel_up[:, :, lo : lo + CHUNK]
+            else:
+                fuel_up_chunk = tanh_logit[c - 2][:]
+                entries = uw_list[:, lo // PER_COLUMN : (lo + CHUNK) // PER_COLUMN]
+                for t in range(PLANES):
+                    nc.scalar.activation(fuel_up_chunk[:, t, :], fuel_plus[:, t, :].indirect(entries), ACT.Copy)
+            miss5 = keep.tile([P, PLANES, CHUNK], F32, name="miss5_%d" % c)
+            both5 = keep.tile([P, PLANES, CHUNK], F32, name="both5_%d" % c)
+            minus5 = keep.tile([P, PLANES, CHUNK], F32, name="minus5_%d" % c)
+            hid = keep.tile([P, CHUNK, PLANES], BF16, name="hid%d" % c, align_bytes=64)
+            hid_words = keep.tile([P, CHUNK], U32, name="hid_words%d" % c, align_bytes=64)
+            hid_scales = keep.tile([P, CHUNK], U8, name="hid_scales%d" % c, align_bytes=64)
+            result = keep.tile([P, N // P, CHUNK], F32, name="result%d" % c)
+            for begin, end in ((0, LEAD), (LEAD, CHUNK)) if c == 0 else ((0, CHUNK),):
+                nc.scalar.activation(
+                    tanh_logit[c][:, :, begin:end], logit[:, :, lo + begin : lo + end], ACT.Tanh, scale=0.5
+                )
+                nc.scalar.activation(
+                    miss5[:, :, begin:end],
+                    tanh_logit[c][:, :, begin:end],
+                    ACT.Exp,
+                    bias=math.log(5.0) - 0.5 / 0.3,
+                    scale=-0.5 / 0.3,
+                )
+                nc.vector.scalar_tensor_tensor(
+                    both5[:, :, begin:end],
+                    th[:, :, lo + begin : lo + end],
+                    2.5,
+                    miss5[:, :, begin:end],
+                    ALU.mult,
+                    ALU.add,
+                )
+                nc.vector.scalar_tensor_tensor(
+                    minus5[:, :, begin:end],
+                    both5[:, :, begin:end],
+                    2.5,
+                    fuel_up_chunk[:, :, begin:end],
+                    ALU.min,
+                    ALU.subtract,
+                )
             nc.vector.tensor_tensor(
-                hid[:].rearrange("p (c i) t -> p c t i", i=4),
-                total[:].rearrange("p t (c i) -> p c t i", i=4),
-                gain[:].unsqueeze(1).unsqueeze(3).to_broadcast([P, w // 4, PACK, 4]),
+                hid[:].rearrange("p (g i) t -> p g t i", i=4),
+                minus5[:].rearrange("p t (g i) -> p g t i", i=4),
+                gain[:].unsqueeze(1).unsqueeze(3).to_broadcast([P, CHUNK // 4, PLANES, 4]),
                 ALU.mult,
             )
-            nc.vector.quantize_mx(out=codes[:].bitcast(FP8X4), scales=scales[:], in_=hid[:].rearrange("p c t -> p (c t)"))
-            acc = psum.tile([P, N // P, w], F32, name="acc%d" % c, tag="bank%d" % c)
+            nc.vector.quantize_mx(
+                out=hid_words[:].bitcast(FP8X4), scales=hid_scales[:], in_=hid[:].rearrange("p n t -> p (n t)")
+            )
+            acc = psum.tile([P, N // P, CHUNK], F32, name="acc%d" % c, tag="bank%d" % (PLANES * WIND + c))
             for a in range(N // P):
                 nc.tensor.matmul_mx(
                     out=acc[:, a, :],
-                    lhsT=w3w[:, 2 * P * a : 2 * P * (a + 1)].bitcast(FP4X4),
-                    lhsT_scale=w3s[:, P * a : P * (a + 1)],
-                    rhs=codes[:].bitcast(FP8X4),
-                    rhs_scale=scales[:],
+                    lhsT=w3_word_tile[:, 2 * P * a : 2 * P * (a + 1)].bitcast(FP4X4),
+                    lhsT_scale=w3_scale_tile[:, P * a : P * (a + 1)],
+                    rhs=hid_words[:].bitcast(FP8X4),
+                    rhs_scale=hid_scales[:],
                     start=True,
                     stop=True,
                 )
-            nc.scalar.copy(res[:], acc[:])
-            nc.sync.dma_start(out=out_rows[:, :, lo:hi], in_=res[:])
+            nc.scalar.copy(result[:], acc[:])
+            nc.sync.dma_start(out=out_rows[:, :, lo : lo + CHUNK], in_=result[:])

import math
from contextlib import ExitStack

import concourse.mybir as mybir

K, T, S, N, H = 512, 2048, 512, 256, 512
FLOPS = 2 * K * H * S * 2 + 2 * H * N * S

F32 = mybir.dt.float32
BF16 = mybir.dt.bfloat16
I32 = mybir.dt.int32
U32 = mybir.dt.uint32
U16 = mybir.dt.uint16
U8 = mybir.dt.uint8
FP8X4 = mybir.dt.float8_e4m3fn_x4
FP4X4 = mybir.dt.float4_e2m1fn_x4
ALU = mybir.AluOpType
ACT = mybir.ActivationFunctionType

P = 128
PLANES = 4
QUADRANTS = 4
PER_COLUMN = 16
WIND, FUEL = 0, 1

SPARE = 8
CHUNK = 128
CHUNKS = S // CHUNK
LEAD = CHUNK // 2
SIDE_PLANES_ON_SCALAR = 3
FUEL_CELLS_ON_VECTOR = S - CHUNK

TINY = 2.0 ** -60
HUGE = 2.0 ** 60


def tile_picked_yfirefr_new_p_kernel(
    tc, x_words, x_scales, w1_words, w1_scales, w2_words, w2_scales, ign, unit, w3_words, w3_scales, offs, uw, sd, out
):
    nc = tc.nc
    with ExitStack() as ctx:
        keep = ctx.enter_context(tc.tile_pool(name="keep", bufs=1))
        psum = ctx.enter_context(tc.psum_pool(name="psum", bufs=1))
        reuse = ctx.enter_context(tc.tile_pool(name="reuse", bufs=1))

        def load_scale_rows(scale_tile, rows, quadrants):
            for q in quadrants:
                nc.sync.dma_start(
                    out=scale_tile[32 * q : 32 * q + 4, :].bitcast(I32), in_=rows[0, 4 * q : 4 * q + 4, :].bitcast(I32)
                )

        offs_list = keep.tile([P, S // PER_COLUMN], U16, name="offs_list")
        uw_list = keep.tile([P, S // PER_COLUMN], U16, name="uw_list")
        sd_list = keep.tile([P, S // PER_COLUMN], U16, name="sd_list")

        x_word_table = reuse.tile([P, T], I32, name="x_word_table", offset=0, align_bytes=64)
        x_scale_table = keep.tile([P, T], U8, name="x_scale_table", align_bytes=64)
        w_words = [keep.tile([P, 2 * H], U8, name="w_words%d" % i, align_bytes=64) for i in (WIND, FUEL)]
        w_scales = [
            keep.tile([P, H], U8, name="w_scales%d" % i, tag="w_scales%d" % i, align_bytes=64) for i in (WIND, FUEL)
        ]
        w3_word_tile = keep.tile([P, 2 * N], U8, name="w3_word_tile", align_bytes=64)
        w3_scale_tile = keep.tile([P, N], U8, name="w3_scale_tile", align_bytes=64)
        ign_pair = [keep.tile([P, 2, S], F32, name="ign_pair%d" % i) for i in range(2)]
        unit_tile = keep.tile([P, PLANES], F32, name="unit_tile")
        burn = [keep.tile([P, S + SPARE], F32, name="burn%d" % t) for t in range(PLANES)]

        nc.gpsimd.memset(x_scale_table[:].bitcast(I32), 0)
        nc.vector.memset(w_scales[WIND][:].bitcast(I32), 0)
        nc.vector.memset(w_scales[FUEL][:].bitcast(I32), 0)
        nc.vector.memset(w3_scale_tile[:].bitcast(I32), 0)
        for t in range(PLANES):
            nc.vector.memset(burn[t][:, S:], 0.0)

        ign_planes = ign.rearrange("(p t) s -> p t s", t=PLANES)
        nc.sync.dma_start(offs_list[:], offs)
        nc.sync.dma_start(out=w_words[WIND][:], in_=w2_words[0])
        nc.sync.dma_start(sd_list[:], sd)
        nc.sync.dma_start(uw_list[:], uw)
        nc.sync.dma_start(out=unit_tile[:], in_=unit.rearrange("(p t) o -> p (t o)", t=PLANES))
        nc.sync.dma_start(out=w_words[FUEL][:], in_=w1_words[0])
        nc.sync.dma_start(out=ign_pair[0][:], in_=ign_planes[:, 0:2, :])
        nc.sync.dma_start(out=ign_pair[1][:], in_=ign_planes[:, 2:4, :])
        load_scale_rows(x_scale_table, x_scales, range(QUADRANTS))
        load_scale_rows(w_scales[WIND], w2_scales, range(1))
        nc.sync.dma_start(out=x_word_table[:], in_=x_words[0].rearrange("p n t -> p (n t)").bitcast(I32))
        load_scale_rows(w_scales[WIND], w2_scales, range(1, QUADRANTS))
        load_scale_rows(w_scales[FUEL], w1_scales, range(QUADRANTS))
        nc.sync.dma_start(out=w3_word_tile[:], in_=w3_words[0])
        load_scale_rows(w3_scale_tile, w3_scales, range(QUADRANTS))

        th = keep.tile([P, PLANES, S], F32, name="th")
        th_flat = th[:].rearrange("p t s -> p (t s)")
        side = [keep.tile([P, S], F32, name="side%d" % t) for t in range(SIDE_PLANES_ON_SCALAR)]
        for i in range(2):
            nc.scalar.activation(th[:, 2 * i : 2 * i + 2, :], ign_pair[i][:], ACT.Tanh, scale=0.5)
        for t in range(SIDE_PLANES_ON_SCALAR):
            window = th_flat[:, S * t : S * (t + 2)]
            nc.scalar.activation(side[t][:], window.indirect(sd_list[:]), ACT.Copy, bias=0.5, scale=0.5)

        dealt_words = [keep.tile([P, 2 * H], U8, name="dealt_words%d" % i, align_bytes=64) for i in (WIND, FUEL)]
        dealt_scales = {}
        cell_words = keep.tile([P, S], U32, name="cell_words", align_bytes=64)
        cell_scales = keep.tile([P, S], U8, name="cell_scales", align_bytes=64)

        def deal_words(i):
            nc.vector.tensor_copy(
                out=dealt_words[i][:].rearrange("p (t m b) -> p m t b", t=PLANES, b=2),
                in_=w_words[i][:].rearrange("p (m t b) -> p m t b", t=PLANES, b=2),
            )

        def deal_scales(i, first, count, dealt):
            nc.vector.tensor_copy(
                out=dealt[:].rearrange("p t m -> p m t"),
                in_=w_scales[i][:].rearrange("p (m t) -> p m t", t=PLANES)[:, :, first : first + count],
            )
            for t in range(count):
                dealt_scales.setdefault((i, first + t), dealt[:, t, :])

        deal_words(WIND)
        nc.vector.tensor_copy(cell_scales[:], x_scale_table[:].indirect(offs_list[:]))
        for t in range(PLANES):
            nc.vector.tensor_scalar(burn[t][:, :S], th[:, t, :], 0.5, 0.5, ALU.mult, ALU.add)
        deal_words(FUEL)
        nc.vector.tensor_copy(cell_words[:], x_word_table[:].bitcast(U32).indirect(offs_list[:]))
        deal_scales(WIND, 0, 2, keep.tile([P, 2, P], U8, name="wind_scales_first", align_bytes=64))
        deal_scales(FUEL, 0, PLANES, reuse.tile([P, PLANES, P], U8, name="fuel_scales", offset=0, align_bytes=64))
        deal_scales(
            WIND, 2, 2, keep.tile([P, 2, P], U8, name="wind_scales_last", tag="w_scales%d" % FUEL, align_bytes=64)
        )

        def first_product(i, t):
            bank = "bank%d" % (PLANES * i + t)
            acc = psum.tile([P, S], F32, name=bank, tag=bank)
            nc.tensor.matmul_mx(
                out=acc[:],
                lhsT=dealt_words[i][:, 2 * P * t : 2 * P * (t + 1)].bitcast(FP4X4),
                lhsT_scale=dealt_scales[(i, t)],
                rhs=cell_words[:].bitcast(FP8X4),
                rhs_scale=cell_scales[:],
                start=True,
                stop=True,
            )
            return acc

        wd = [first_product(WIND, t) for t in range(2)]
        fu = [first_product(FUEL, t) for t in range(PLANES)]
        wd.extend([first_product(WIND, t) for t in range(2, PLANES)])

        gain = keep.tile([P, PLANES], F32, name="gain")
        nc.vector.tensor_scalar(gain[:], unit_tile[:], -0.2, None, ALU.mult)

        tanh_wd = keep.tile([P, PLANES, S], F32, name="tanh_wd", tag="tanh_wd")
        wind2 = keep.tile([P, PLANES, S], F32, name="wind2", tag="wind2")
        upwind = keep.tile([P, PLANES, S], F32, name="upwind")
        heat2 = keep.tile([P, PLANES, S], F32, name="heat2")

        def heat_plane(t):
            nc.scalar.activation(tanh_wd[:, t, :], wd[t][:], ACT.Tanh)
            nc.scalar.activation(wind2[:, t, :], tanh_wd[:, t, :], ACT.Exp, bias=math.log(2.0), scale=0.9)
            nc.vector.tensor_tensor(upwind[:, t, :], burn[t][:].indirect(uw_list[:]), wind2[:, t, :], ALU.mult)
            if t < SIDE_PLANES_ON_SCALAR:
                nc.vector.tensor_tensor(heat2[:, t, :], upwind[:, t, :], side[t][:], ALU.add)
            else:
                nc.vector.tensor_tensor(heat2[:, t, :], burn[t][:].indirect(sd_list[:]), upwind[:, t, :], ALU.add)

        exp_fu = keep.tile([P, PLANES, S], F32, name="exp_fu")
        exp_fu_bounded = keep.tile([P, PLANES, S], F32, name="exp_fu_bounded")
        fuel_plus = keep.tile([P, PLANES, S], F32, name="fuel_plus")
        log_fuel = keep.tile([P, PLANES, S], F32, name="log_fuel")
        fuel_up = keep.tile([P, PLANES, FUEL_CELLS_ON_VECTOR], F32, name="fuel_up")

        heat_plane(0)
        heat_plane(1)
        for t in range(PLANES):
            nc.scalar.activation(exp_fu[:, t, :], fu[t][:], ACT.Exp)
        nc.vector.tensor_scalar(exp_fu_bounded[:], exp_fu[:], HUGE, None, ALU.min)
        heat_plane(2)
        heat_plane(3)

        soft_plus = keep.tile([P, PLANES, S], F32, name="soft_plus", tag="tanh_wd")
        log_heat = keep.tile([P, PLANES, S], F32, name="log_heat", tag="wind2")
        for t in range(PLANES):
            nc.scalar.activation(
                soft_plus[:, t, :], exp_fu_bounded[:, t, :], ACT.Ln, bias=math.exp(2.6), scale=math.exp(2.6)
            )
            nc.vector.scalar_tensor_tensor(fuel_plus[:, t, :], fu[t][:], 2.6, soft_plus[:, t, :], ALU.add, ALU.max)
        for t in range(PLANES):
            nc.scalar.activation(log_heat[:, t, :], heat2[:, t, :], ACT.Ln, bias=TINY, scale=0.15)
        for t in range(PLANES):
            nc.scalar.activation(log_fuel[:, t, :], fuel_plus[:, t, :], ACT.Ln, bias=-2.5)
        for t in range(PLANES):
            entries = uw_list[:, : FUEL_CELLS_ON_VECTOR // PER_COLUMN]
            nc.vector.tensor_copy(fuel_up[:, t, :], fuel_plus[:, t, :].indirect(entries))

        logit = keep.tile([P, PLANES, S], F32, name="logit")
        for lo, hi in ((0, LEAD), (LEAD, S // 2), (S // 2, S)):
            nc.vector.tensor_tensor(logit[:, :, lo:hi], log_heat[:, :, lo:hi], log_fuel[:, :, lo:hi], ALU.subtract)

        out_rows = out.rearrange("(a p) s -> p a s", p=P)
        tanh_logit = []
        for c in range(CHUNKS):
            lo = c * CHUNK
            tanh_logit.append(keep.tile([P, PLANES, CHUNK], F32, name="tanh_logit%d" % c))
            if lo < FUEL_CELLS_ON_VECTOR:
                fuel_up_chunk = fuel_up[:, :, lo : lo + CHUNK]
            else:
                fuel_up_chunk = tanh_logit[c - 2][:]
                entries = uw_list[:, lo // PER_COLUMN : (lo + CHUNK) // PER_COLUMN]
                for t in range(PLANES):
                    nc.scalar.activation(fuel_up_chunk[:, t, :], fuel_plus[:, t, :].indirect(entries), ACT.Copy)
            miss5 = keep.tile([P, PLANES, CHUNK], F32, name="miss5_%d" % c)
            both5 = keep.tile([P, PLANES, CHUNK], F32, name="both5_%d" % c)
            minus5 = keep.tile([P, PLANES, CHUNK], F32, name="minus5_%d" % c)
            hid = keep.tile([P, CHUNK, PLANES], BF16, name="hid%d" % c, align_bytes=64)
            hid_words = keep.tile([P, CHUNK], U32, name="hid_words%d" % c, align_bytes=64)
            hid_scales = keep.tile([P, CHUNK], U8, name="hid_scales%d" % c, align_bytes=64)
            result = keep.tile([P, N // P, CHUNK], F32, name="result%d" % c)
            for begin, end in ((0, LEAD), (LEAD, CHUNK)) if c == 0 else ((0, CHUNK),):
                nc.scalar.activation(
                    tanh_logit[c][:, :, begin:end], logit[:, :, lo + begin : lo + end], ACT.Tanh, scale=0.5
                )
                nc.scalar.activation(
                    miss5[:, :, begin:end],
                    tanh_logit[c][:, :, begin:end],
                    ACT.Exp,
                    bias=math.log(5.0) - 0.5 / 0.3,
                    scale=-0.5 / 0.3,
                )
                nc.vector.scalar_tensor_tensor(
                    both5[:, :, begin:end],
                    th[:, :, lo + begin : lo + end],
                    2.5,
                    miss5[:, :, begin:end],
                    ALU.mult,
                    ALU.add,
                )
                nc.vector.scalar_tensor_tensor(
                    minus5[:, :, begin:end],
                    both5[:, :, begin:end],
                    2.5,
                    fuel_up_chunk[:, :, begin:end],
                    ALU.min,
                    ALU.subtract,
                )
            nc.vector.tensor_tensor(
                hid[:].rearrange("p (g i) t -> p g t i", i=4),
                minus5[:].rearrange("p t (g i) -> p g t i", i=4),
                gain[:].unsqueeze(1).unsqueeze(3).to_broadcast([P, CHUNK // 4, PLANES, 4]),
                ALU.mult,
            )
            nc.vector.quantize_mx(
                out=hid_words[:].bitcast(FP8X4), scales=hid_scales[:], in_=hid[:].rearrange("p n t -> p (n t)")
            )
            acc = psum.tile([P, N // P, CHUNK], F32, name="acc%d" % c, tag="bank%d" % (PLANES * WIND + c))
            for a in range(N // P):
                nc.tensor.matmul_mx(
                    out=acc[:, a, :],
                    lhsT=w3_word_tile[:, 2 * P * a : 2 * P * (a + 1)].bitcast(FP4X4),
                    lhsT_scale=w3_scale_tile[:, P * a : P * (a + 1)],
                    rhs=hid_words[:].bitcast(FP8X4),
                    rhs_scale=hid_scales[:],
                    start=True,
                    stop=True,
                )
            nc.scalar.copy(result[:], acc[:])
            nc.sync.dma_start(out=out_rows[:, :, lo : lo + CHUNK], in_=result[:])
